import numpy as np, ml_dtypes
CORES = [21,109,149,237,277,365,405,493,150,406]
N = 10
def setup_inputs(rng):
    dy = rng.standard_normal((N, 128, N * 128), dtype=np.float32).astype(ml_dtypes.bfloat16)
    dyt = np.concatenate([dy[:, :, 128 * j:128 * j + 128].transpose(0, 2, 1) for j in range(N)], axis=2)
    return {"x": rng.standard_normal((N, 128, 128), dtype=np.float32).astype(ml_dtypes.bfloat16), "wt": rng.standard_normal((N, 128, 128), dtype=np.float32).astype(ml_dtypes.bfloat16), "dy": dy, "dyt": dyt}
def setup_inputs_big(rng):
    d = setup_inputs(rng)
    for k in ("x", "wt", "dy", "dyt"): d[k] = (d[k].astype(np.float32) * 1024.0).astype(d[k].dtype)
    return d
def setup_inputs_small(rng):
    d = setup_inputs(rng)
    for k in ("x", "wt", "dy", "dyt"): d[k] = (d[k].astype(np.float32) * (1 / 1024.0)).astype(d[k].dtype)
    return d
def setup_inputs_apart(rng):
    d = setup_inputs(rng)
    f = (10.0 ** rng.permutation(np.linspace(-1.5, 1.5, N))).astype(np.float32).reshape(N, 1, 1)
    for k in ("x", "wt", "dy", "dyt"): d[k] = (d[k].astype(np.float32) * f).astype(d[k].dtype)
    return d
def tie_inputs(x):
    x = dict(x)
    x["dyt"] = np.concatenate([x["dy"][:, :, 128 * j:128 * j + 128].transpose(0, 2, 1) for j in range(N)], axis=2)
    return x
def reference(x, wt, dy, dyt):
    X, WT, DY, DYT = x.astype(np.float64), wt.astype(np.float64), dy.astype(np.float64), dyt.astype(np.float64)
    dx = np.zeros((N, 128, 128)); dw = np.zeros((N, 128, 128))
    for r in range(N):
        for j in range(N):
            dx[r] += WT[j].T @ DY[j][:, 128 * r:128 * r + 128]
            dw[r] += X[j].T @ DYT[r][:, 128 * j:128 * j + 128]
    return {"dx": dx.astype(ml_dtypes.bfloat16 if x.dtype != np.float64 else np.float64), "dw": dw.astype(ml_dtypes.bfloat16 if x.dtype != np.float64 else np.float64)}

@@ -1,0 +1,269 @@
+from concourse.bass import DstId, RemoteDMATransfer
+from concourse.mybir import AluOpType
+
+N = 10
+B = 128
+W3 = 3 * B
+
+SCRATCH = {
+    "xs": ("sbuf", [128, B], "bfloat16"),
+    "wts": ("sbuf", [128, B], "bfloat16"),
+    "dys": ("sbuf", [128, N * B], "bfloat16"),
+    "dyts": ("sbuf", [128, N * B], "bfloat16"),
+    "xg": ("sbuf", [128, N * B], "bfloat16"),
+    "pbs": ("sbuf", [128, 9 * B], "bfloat16"),
+    "pl": ("sbuf", [128, 4 * B], "bfloat16"),
+    "ub": ("sbuf", [128, 3 * B], "bfloat16"),
+    "upb": ("sbuf", [128, 9 * B], "bfloat16"),
+    "dxo": ("sbuf", [128, B], "bfloat16"),
+    "dwo": ("sbuf", [128, B], "bfloat16"),
+    "pb0": ("psum", [128, 512], "float32"),
+    "pb1": ("psum", [128, 512], "float32"),
+    "pb2": ("psum", [128, 512], "float32"),
+    "pacc": ("psum", [128, 512], "float32"),
+    "pdw": ("psum", [128, 512], "float32"),
+}
+SEMAPHORES = ["lx", "lw", "ld0", "ld1", "lt0", "lt1", "mb0", "mb1", "mb2", "mo", "md", "vc", "vd", "va",
+              "xr0", "xr1", "xr2", "xr3", "pr0", "pr1", "pr2", "pr3", "ux", "up", "sent", "sdw", "sdx"]
+
+_CACHE = {}
+
+
+def _bits(mask):
+    return [b for b in range(32) if (mask >> b) & 1]
+
+
+def _mk(bits):
+    m = 0
+    for b in bits:
+        m |= 1 << b
+    return m
+
+
+def _plan(cores, topo):
+    key = tuple(cores)
+    if key in _CACHE:
+        return _CACHE[key]
+    ranks = list(cores)
+    hosts = sorted(set(topo.host(c) for c in ranks))
+    world = range((max(hosts) + 1) * topo.CORES_PER_HOST)
+    chips = sorted(set(topo.chip(c) for c in ranks))
+
+    def on(h, q):
+        return [c for c in ranks if topo.host(c) == h and topo.chip(c) == chips[q]]
+
+    def inhost(h):
+        return [c for c in ranks if topo.host(c) == h]
+
+    def rackmate(h):
+        return [k for k in hosts if k != h and topo.rack(k) == topo.rack(h)][0]
+
+    def cabled(h):
+        return [k for k in hosts if topo.rack(k) != topo.rack(h) and topo.may_write(inhost(h)[0], inhost(k)[0])][0]
+
+    def pos(h):
+        return 0 if len(inhost(h)) < len(inhost(rackmate(h))) else 1
+
+    relay = {}
+    for h in hosts:
+        for q in (0, 1):
+            other = on(h, 1 - q)[0]
+            mine = on(h, q)[0]
+            cand = [c for c in world if topo.host(c) == h and topo.chip(c) == chips[q] and c not in ranks
+                    and topo.may_write(c, other)]
+            relay[(h, q, "A")] = [c for c in cand if topo.die(c) == topo.die(mine)][0]
+            relay[(h, q, "B")] = [c for c in cand if topo.die(c) != topo.die(mine)][0]
+
+    arr = {}
+    calls = {}
+
+    def add(core, kind, transfers):
+        calls.setdefault(core, []).append((kind, transfers))
+        for t in transfers:
+            n = len(_bits(t["mask"]))
+            for d in t["to"]:
+                arr[(d, t["sem"])] = arr.get((d, t["sem"]), 0) + n
+            arr[(core, "sent")] = arr.get((core, "sent"), 0) + n
+
+    def lanes(core, dests):
+        m = ~0
+        for d in dests:
+            m &= topo.mask(core, d)
+        return m
+
+    xsrc = {}
+    for h in hosts:
+        for q in (0, 1):
+            xsrc[(h, q)] = on(h, q) + on(cabled(h), q)
+    width = [len(xsrc[(hosts[0], q)]) for q in (0, 1)]
+    xoff = [0, width[0] * B, 2 * width[0] * B, (2 * width[0] + width[1]) * B]
+
+    units = []
+    for h in hosts:
+        if pos(h) != 0:
+            continue
+        e, o = h, rackmate(h)
+        for q in (0, 1):
+            srcs = on(e, q) + on(o, q)
+            near = [c for c in inhost(e) + inhost(o) if c not in srcs]
+            big = len(srcs) > 2
+            extra = [c for c in near if topo.host(c) == (o if big else e)][0]
+            u3 = srcs + [c for c in near if c != extra]
+            units.append({"core": relay[(e, q, "B")], "srcs": srcs, "dests": inhost(cabled(e)), "q": q})
+            units.append({"core": relay[(o, q, "B" if big else "A")], "srcs": srcs, "dests": inhost(cabled(o)) + [extra], "q": q})
+            units.append({"core": relay[(o if big else e, q, "A")], "srcs": srcs, "dests": u3, "q": q})
+
+    info = {}
+    for c in ranks:
+        h, q = topo.host(c), chips.index(topo.chip(c))
+        far = cabled(h)
+        offm = lanes(c, [relay[(far, q, "A")]])
+        onm = lanes(c, [relay[(h, q, "A")]]) & ~offm
+        add(c, "x", [
+            {"srcs": [("xs", 0, B)], "to": [relay[(far, q, "A")], relay[(far, q, "B")]],
+             "dst": ("ub", xsrc[(far, q)].index(c) * B, B), "mask": offm, "sem": "ux"},
+            {"srcs": [("xs", 0, B)], "to": [relay[(h, q, "A")], relay[(h, q, "B")]],
+             "dst": ("ub", xsrc[(h, q)].index(c) * B, B), "mask": onm, "sem": "ux"},
+        ])
+        mine = [u for u in units if c in u["srcs"]]
+        bundles = [[d for d in u["dests"] if d != c] for u in mine]
+        same = [topo.host(u["core"]) == h and topo.chip(u["core"]) == topo.chip(c) for u in mine]
+        trs = []
+        for grp, m in ((False, offm), (True, onm)):
+            ks = [k for k in range(len(mine)) if same[k] == grp]
+            bl = _bits(m)
+            per = len(bl) // (1 if len(ks) == 1 else 2)
+            for i, k in enumerate(ks):
+                trs.append({"srcs": [("pbs", k * W3, W3)], "to": [mine[k]["core"]],
+                            "dst": ("upb", mine[k]["srcs"].index(c) * W3, W3),
+                            "mask": _mk(bl[i * per:(i + 1) * per]), "sem": "up"})
+        add(c, "p", trs)
+        info[c] = {"bundles": bundles}
+
+    for h in hosts:
+        for q in (0, 1):
+            k = 2 * q + pos(h)
+            w = len(xsrc[(h, q)]) * B
+            for ab, dq in (("A", q), ("B", 1 - q)):
+                rc = relay[(h, q, ab)]
+                to = on(rackmate(h), dq) + on(h, dq)
+                add(rc, "x", [{"srcs": [("ub", 0, w)], "to": to, "dst": ("xg", xoff[k], w),
+                               "mask": lanes(rc, to), "sem": "xr%d" % k}])
+    for u in units:
+        rc = u["core"]
+        bl = _bits(lanes(rc, u["dests"]))
+        share = [4, 2, 2] if len(u["dests"]) == 3 else [2, 2, 2, 2]
+        trs, at = [], 0
+        for i, d in enumerate(u["dests"]):
+            srcs = []
+            for si, s in enumerate(u["srcs"]):
+                if s != d:
+                    srcs.append(("upb", si * W3 + [x for x in u["dests"] if x != s].index(d) * B, B))
+            slot = 2 * (1 if topo.rack(topo.host(d)) == topo.rack(topo.host(rc)) else 0) + u["q"]
+            trs.append({"srcs": srcs, "to": [d], "dst": ("pl", slot * B, B),
+                        "mask": _mk(bl[at:at + share[i]]), "sem": "pr%d" % slot})
+            at += share[i]
+        add(rc, "p", trs)
+
+    for c in ranks:
+        h, q = topo.host(c), chips.index(topo.chip(c))
+        groups = []
+        for (hh, qq) in ((h, q), (rackmate(h), q), (h, 1 - q), (rackmate(h), 1 - q)):
+            k = 2 * qq + pos(hh)
+            groups.append(("xr%d" % k, [(ranks.index(s), xoff[k] + i * B) for i, s in enumerate(xsrc[(hh, qq)]) if s != c]))
+        info[c]["xgroups"] = groups
+    out = {"calls": calls, "arr": arr, "info": info}
+    _CACHE[key] = out
+    return out
+
+
+def _ap(T, spec):
+    buf, c0, n = spec
+    return T[buf][:, c0:c0 + n]
+
+
+def _issue(g, core, T, topo, transfers):
+    out = []
+    for t in transfers:
+        ids = []
+        for d in t["to"]:
+            rid, pid = topo.addr(d, core)
+            ids.append(DstId(rid=rid, pnc=pid))
+        out.append(RemoteDMATransfer(dst_ids=ids, dma_engine_mask=t["mask"], remote_sem=T.sem[t["sem"]],
+                                     srcs=[_ap(T, s) for s in t["srcs"]], dsts=[_ap(T, t["dst"]) for _ in t["to"]],
+                                     alu_op=1 if len(t["srcs"]) > 1 else 0))
+    g.remote_dma_fused(out, local_sem=T.sem.sent)
+
+
+def rank_program(g, core, T, topo):
+    plan = _plan(T.cores, topo)
+    calls = plan["calls"].get(core)
+    if calls is None:
+        return
+    arr, S = plan["arr"], T.sem
+    r = T.rank_of(core)
+
+    if r is None:
+        for kind, trs in calls:
+            sem = "ux" if kind == "x" else "up"
+            g.wait_ge(S[sem], arr[(core, sem)])
+            _issue(g, core, T, topo, trs)
+        g.wait_ge(S.sent, arr[(core, "sent")])
+        return
+
+    info = plan["info"][core]
+    sy, sc, te, ve = g.sync, g.scalar, g.tensor, g.vector
+    H = (N // 2) * B
+
+    sy.dma_start(T.xs[:], T.x[:]).then_inc(S.lx, 16)
+    sc.dma_start(T.wts[:], T.wt[:]).then_inc(S.lw, 16)
+    sy.dma_start(T.dys[:, 0:H], T.dy[:, 0:H]).then_inc(S.ld0, 16)
+    sc.dma_start(T.dys[:, H:N * B], T.dy[:, H:N * B]).then_inc(S.ld1, 16)
+    sy.dma_start(T.dyts[:, 0:H], T.dyt[:, 0:H]).then_inc(S.lt0, 16)
+    sc.dma_start(T.dyts[:, H:N * B], T.dyt[:, H:N * B]).then_inc(S.lt1, 16)
+
+    g.wait_ge(S.lx, 16)
+    _issue(g, core, T, topo, calls[0][1])
+    g.wait_ge(S.vc, 3)
+    _issue(g, core, T, topo, calls[1][1])
+
+    te.wait_ge(S.lw, 16)
+    te.wait_ge(S.ld0, 16)
+    te.wait_ge(S.ld1, 16)
+    for k, bun in enumerate(info["bundles"]):
+        for i, d in enumerate(bun):
+            j = T.rank_of(d)
+            te.matmul(T["pb%d" % k][:, i * B:(i + 1) * B], T.wts[:], T.dys[:, j * B:(j + 1) * B], True, True).then_inc(S["mb%d" % k], 1)
+    te.matmul(T.pacc[:, 0:B], T.wts[:], T.dys[:, r * B:(r + 1) * B], True, True).then_inc(S.mo, 1)
+    te.wait_ge(S.lx, 16)
+    te.wait_ge(S.lt0, 16)
+    te.wait_ge(S.lt1, 16)
+    te.matmul(T.pdw[:, 0:B], T.xs[:], T.dyts[:, r * B:(r + 1) * B], True, False).then_inc(S.md, 1)
+    left = N - 1
+    for sem, parts in info["xgroups"]:
+        te.wait_ge(S[sem], arr[(core, sem)])
+        for j, col in parts:
+            left -= 1
+            te.matmul(T.pdw[:, 0:B], T.xg[:, col:col + B], T.dyts[:, j * B:(j + 1) * B], False, left == 0).then_inc(S.md, 1)
+
+    for k in range(3):
+        ve.wait_ge(S["mb%d" % k], 3)
+        ve.tensor_copy(T.pbs[:, k * W3:(k + 1) * W3], T["pb%d" % k][:, 0:W3]).then_inc(S.vc, 1)
+    ve.wait_ge(S.md, N)
+    ve.tensor_copy(T.dwo[:], T.pdw[:, 0:B]).then_inc(S.vd, 1)
+    ve.wait_ge(S.mo, 1)
+    for i, slot in enumerate((2, 3, 0, 1)):
+        sem = "pr%d" % slot
+        ve.wait_ge(S[sem], arr[(core, sem)])
+        if i:
+            ve.wait_ge(S.va, i)
+        dst = T.dxo[:] if i == 3 else T.pacc[:, (i + 1) * B:(i + 2) * B]
+        ve.tensor_tensor(dst, T.pacc[:, i * B:(i + 1) * B], T.pl[:, slot * B:(slot + 1) * B], AluOpType.add).then_inc(S.va, 1)
+
+    sy.wait_ge(S.vd, 1)
+    sy.dma_start(T.dw[:], T.dwo[:]).then_inc(S.sdw, 16)
+    sy.wait_ge(S.sdw, 16)
+    sc.wait_ge(S.va, 4)
+    sc.dma_start(T.dx[:], T.dxo[:]).then_inc(S.sdx, 16)
+    sc.wait_ge(S.sdx, 16)
+    g.wait_ge(S.sent, arr[(core, "sent")])

@@ -23,8 +23,9 @@ SCRATCH = {
     "pacc": ("psum", [128, 512], "float32"),
     "pdw": ("psum", [128, 512], "float32"),
 }
-SEMAPHORES = ["lx", "lw", "ld0", "ld1", "lt0", "lt1", "mb0", "mb1", "mb2", "mo", "md", "vc", "vd", "va",
-              "xr0", "xr1", "xr2", "xr3", "pr0", "pr1", "pr2", "pr3", "ux", "up", "sent", "sdw", "sdx"]
+SEMAPHORES = ["lx", "lw", "ld0", "ld1", "lt0", "lt1", "mb0", "mb1", "mb2", "mo", "md", "vc", "vc2", "vd", "va",
+              "xr0", "xr1", "xr2", "xr3", "xf0", "xf1", "xf2", "xf3", "pr0", "pr1", "pr2", "pr3",
+              "ux", "uy", "up", "sent", "sdw", "sdx"]
 
 _CACHE = {}
 
@@ -77,8 +78,8 @@ def _plan(cores, topo):
     arr = {}
     calls = {}
 
-    def add(core, kind, transfers):
-        calls.setdefault(core, []).append((kind, transfers))
+    def add(core, wait, transfers):
+        calls.setdefault(core, []).append((wait, transfers))
         for t in transfers:
             n = len(_bits(t["mask"]))
             for d in t["to"]:
@@ -91,86 +92,109 @@ def _plan(cores, topo):
             m &= topo.mask(core, d)
         return m
 
+    def split(core, dests):
+        onc = [d for d in dests if topo.host(d) == topo.host(core) and topo.chip(d) == topo.chip(core)]
+        off = [d for d in dests if d not in onc]
+        lo = lanes(core, off)
+        hi = (lanes(core, onc) & ~lo) if onc else 0
+        return off, onc, _bits(lo), _bits(hi)
+
     xsrc = {}
     for h in hosts:
         for q in (0, 1):
             xsrc[(h, q)] = on(h, q) + on(cabled(h), q)
     width = [len(xsrc[(hosts[0], q)]) for q in (0, 1)]
     xoff = [0, width[0] * B, 2 * width[0] * B, (2 * width[0] + width[1]) * B]
+    xunits = []
+    for h in hosts:
+        for q in (0, 1):
+            oth = on(rackmate(h), 1 - q) + on(h, 1 - q)
+            moved = [c for c in oth if pos(topo.host(c)) == 0] if len(oth) > 2 else []
+            for ab, to in (("A", on(rackmate(h), q) + moved + on(h, q)), ("B", [c for c in oth if c not in moved])):
+                xunits.append({"core": relay[(h, q, ab)], "srcs": xsrc[(h, q)], "dests": to, "k": 2 * q + pos(h)})
 
     units = []
-    for h in hosts:
-        if pos(h) != 0:
+    for e in hosts:
+        if pos(e) != 0:
             continue
-        e, o = h, rackmate(h)
+        o = rackmate(e)
         for q in (0, 1):
             srcs = on(e, q) + on(o, q)
-            near = [c for c in inhost(e) + inhost(o) if c not in srcs]
-            big = len(srcs) > 2
-            extra = [c for c in near if topo.host(c) == (o if big else e)][0]
-            u3 = srcs + [c for c in near if c != extra]
-            units.append({"core": relay[(e, q, "B")], "srcs": srcs, "dests": inhost(cabled(e)), "q": q})
-            units.append({"core": relay[(o, q, "B" if big else "A")], "srcs": srcs, "dests": inhost(cabled(o)) + [extra], "q": q})
-            units.append({"core": relay[(o if big else e, q, "A")], "srcs": srcs, "dests": u3, "q": q})
+            fe, fo = inhost(cabled(e)), inhost(cabled(o))
+            ne = [c for c in inhost(e) if c not in srcs]
+            no = [c for c in inhost(o) if c not in srcs]
+            two = len(on(o, q)) > 1
+            for hh, ab, to in ((e, "B", fe[0:2]), (e, "A", fe[2:] + ne + ([] if two else on(e, q))),
+                               (o, "B", fo[0:1] + no[0:1]), (o, "A", fo[1:] + no[1:] + (on(e, q) if two else []) + on(o, q))):
+                units.append({"core": relay[(hh, q, ab)], "srcs": srcs, "dests": to, "q": q})
 
     info = {}
     for c in ranks:
         h, q = topo.host(c), chips.index(topo.chip(c))
         far = cabled(h)
-        offm = lanes(c, [relay[(far, q, "A")]])
-        onm = lanes(c, [relay[(h, q, "A")]]) & ~offm
-        add(c, "x", [
-            {"srcs": [("xs", 0, B)], "to": [relay[(far, q, "A")], relay[(far, q, "B")]],
-             "dst": ("ub", xsrc[(far, q)].index(c) * B, B), "mask": offm, "sem": "ux"},
-            {"srcs": [("xs", 0, B)], "to": [relay[(h, q, "A")], relay[(h, q, "B")]],
-             "dst": ("ub", xsrc[(h, q)].index(c) * B, B), "mask": onm, "sem": "ux"},
+        xto = [relay[(far, q, "A")], relay[(far, q, "B")], relay[(h, q, "A")], relay[(h, q, "B")]]
+        off, onc, lo, hi = split(c, xto)
+        add(c, None, [
+            {"srcs": [("xs", 0, B)], "to": off, "dst": ("ub", xsrc[(far, q)].index(c) * B, B), "mask": _mk(lo), "sem": "uy"},
+            {"srcs": [("xs", 0, B)], "to": onc, "dst": ("ub", xsrc[(h, q)].index(c) * B, B), "mask": _mk(hi), "sem": "ux"},
         ])
         mine = [u for u in units if c in u["srcs"]]
+        mine.sort(key=lambda u: len([d for d in u["dests"] if d != c]))
         bundles = [[d for d in u["dests"] if d != c] for u in mine]
-        same = [topo.host(u["core"]) == h and topo.chip(u["core"]) == topo.chip(c) for u in mine]
-        trs = []
-        for grp, m in ((False, offm), (True, onm)):
-            ks = [k for k in range(len(mine)) if same[k] == grp]
-            bl = _bits(m)
-            per = len(bl) // (1 if len(ks) == 1 else 2)
-            for i, k in enumerate(ks):
-                trs.append({"srcs": [("pbs", k * W3, W3)], "to": [mine[k]["core"]],
-                            "dst": ("upb", mine[k]["srcs"].index(c) * W3, W3),
-                            "mask": _mk(bl[i * per:(i + 1) * per]), "sem": "up"})
-        add(c, "p", trs)
-        info[c] = {"bundles": bundles}
+        start = [sum(len(b) for b in bundles[:k]) * B for k in range(len(mine))]
+        for wd in sorted(set(len(b) for b in bundles)):
+            trs = []
+            for grp, bl in ((False, lo), (True, hi)):
+                ks = [k for k in range(len(mine)) if (mine[k]["core"] in onc) == grp and len(bundles[k]) == wd]
+                for i, k in enumerate(ks):
+                    per = len(bl) // len(ks)
+                    trs.append({"srcs": [("pbs", start[k], wd * B)], "to": [mine[k]["core"]],
+                                "dst": ("upb", mine[k]["srcs"].index(c) * W3, wd * B),
+                                "mask": _mk(bl[i * per:(i + 1) * per]), "sem": "up"})
+            add(c, None, trs)
+        info[c] = {"order": [d for b in bundles for d in b]}
 
-    for h in hosts:
-        for q in (0, 1):
-            k = 2 * q + pos(h)
-            w = len(xsrc[(h, q)]) * B
-            for ab, dq in (("A", q), ("B", 1 - q)):
-                rc = relay[(h, q, ab)]
-                to = on(rackmate(h), dq) + on(h, dq)
-                add(rc, "x", [{"srcs": [("ub", 0, w)], "to": to, "dst": ("xg", xoff[k], w),
-                               "mask": lanes(rc, to), "sem": "xr%d" % k}])
+    for u in xunits:
+        rc, k = u["core"], u["k"]
+        n = len(u["srcs"])
+        own = len([s for s in u["srcs"] if topo.host(s) == topo.host(rc)])
+        off, onc, lo, hi = split(rc, u["dests"])
+        for wait, sem, c0, m in (("ux", "xr%d" % k, 0, own), ("uy", "xf%d" % k, own, n - own)):
+            src, dst = ("ub", c0 * B, m * B), ("xg", xoff[k] + c0 * B, m * B)
+            trs = [{"srcs": [src], "to": off, "dst": dst, "mask": _mk(lo), "sem": sem}]
+            if onc and (wait == "uy" or own > 1):
+                trs.append({"srcs": [src], "to": onc, "dst": dst, "mask": _mk(hi[0:4 * len(onc)]), "sem": sem})
+            add(rc, wait, trs)
     for u in units:
         rc = u["core"]
-        bl = _bits(lanes(rc, u["dests"]))
-        share = [4, 2, 2] if len(u["dests"]) == 3 else [2, 2, 2, 2]
-        trs, at = [], 0
-        for i, d in enumerate(u["dests"]):
+        off, onc, lo, hi = split(rc, u["dests"])
+        per = len(lo) // len(off)
+        trs = []
+        for d in u["dests"]:
             srcs = []
             for si, s in enumerate(u["srcs"]):
                 if s != d:
                     srcs.append(("upb", si * W3 + [x for x in u["dests"] if x != s].index(d) * B, B))
             slot = 2 * (1 if topo.rack(topo.host(d)) == topo.rack(topo.host(rc)) else 0) + u["q"]
-            trs.append({"srcs": srcs, "to": [d], "dst": ("pl", slot * B, B),
-                        "mask": _mk(bl[at:at + share[i]]), "sem": "pr%d" % slot})
-            at += share[i]
-        add(rc, "p", trs)
+            if d in off:
+                i = off.index(d)
+                m = _mk(lo[i * per:(i + 1) * per])
+            else:
+                i = onc.index(d)
+                m = _mk(hi[4 * i:4 * i + 4])
+            trs.append({"srcs": srcs, "to": [d], "dst": ("pl", slot * B, B), "mask": m, "sem": "pr%d" % slot})
+        add(rc, "up", trs)
 
     for c in ranks:
         h, q = topo.host(c), chips.index(topo.chip(c))
         groups = []
-        for (hh, qq) in ((h, q), (rackmate(h), q), (h, 1 - q), (rackmate(h), 1 - q)):
-            k = 2 * qq + pos(hh)
-            groups.append(("xr%d" % k, [(ranks.index(s), xoff[k] + i * B) for i, s in enumerate(xsrc[(hh, qq)]) if s != c]))
+        for early in (True, False):
+            for (hh, qq) in ((h, q), (rackmate(h), q), (h, 1 - q), (rackmate(h), 1 - q)):
+                k = 2 * qq + pos(hh)
+                parts = [(ranks.index(s), xoff[k] + i * B) for i, s in enumerate(xsrc[(hh, qq)])
+                         if s != c and (topo.host(s) == hh) == early]
+                if parts:
+                    groups.append((("xr%d" if early else "xf%d") % k, parts))
         info[c]["xgroups"] = groups
     out = {"calls": calls, "arr": arr, "info": info}
     _CACHE[key] = out
@@ -204,8 +228,7 @@ def rank_program(g, core, T, topo):
     r = T.rank_of(core)
 
     if r is None:
-        for kind, trs in calls:
-            sem = "ux" if kind == "x" else "up"
+        for sem, trs in calls:
             g.wait_ge(S[sem], arr[(core, sem)])
             _issue(g, core, T, topo, trs)
         g.wait_ge(S.sent, arr[(core, "sent")])
@@ -224,16 +247,17 @@ def rank_program(g, core, T, topo):
 
     g.wait_ge(S.lx, 16)
     _issue(g, core, T, topo, calls[0][1])
-    g.wait_ge(S.vc, 3)
+    g.wait_ge(S.vc, 2)
     _issue(g, core, T, topo, calls[1][1])
+    g.wait_ge(S.vc2, 1)
+    _issue(g, core, T, topo, calls[2][1])
 
     te.wait_ge(S.lw, 16)
     te.wait_ge(S.ld0, 16)
     te.wait_ge(S.ld1, 16)
-    for k, bun in enumerate(info["bundles"]):
-        for i, d in enumerate(bun):
-            j = T.rank_of(d)
-            te.matmul(T["pb%d" % k][:, i * B:(i + 1) * B], T.wts[:], T.dys[:, j * B:(j + 1) * B], True, True).then_inc(S["mb%d" % k], 1)
+    for n, d in enumerate(info["order"]):
+        k, i, j = n // 3, n % 3, T.rank_of(d)
+        te.matmul(T["pb%d" % k][:, i * B:(i + 1) * B], T.wts[:], T.dys[:, j * B:(j + 1) * B], True, True).then_inc(S["mb%d" % k], 1)
     te.matmul(T.pacc[:, 0:B], T.wts[:], T.dys[:, r * B:(r + 1) * B], True, True).then_inc(S.mo, 1)
     te.wait_ge(S.lx, 16)
     te.wait_ge(S.lt0, 16)
@@ -248,7 +272,7 @@ def rank_program(g, core, T, topo):
 
     for k in range(3):
         ve.wait_ge(S["mb%d" % k], 3)
-        ve.tensor_copy(T.pbs[:, k * W3:(k + 1) * W3], T["pb%d" % k][:, 0:W3]).then_inc(S.vc, 1)
+        ve.tensor_copy(T.pbs[:, k * W3:(k + 1) * W3], T["pb%d" % k][:, 0:W3]).then_inc(S.vc if k < 2 else S.vc2, 1)
     ve.wait_ge(S.md, N)
     ve.tensor_copy(T.dwo[:], T.pdw[:, 0:B]).then_inc(S.vd, 1)
     ve.wait_ge(S.mo, 1)

from concourse.bass import DstId, RemoteDMATransfer
from concourse.mybir import AluOpType

N = 10
B = 128
W3 = 3 * B

SCRATCH = {
    "xs": ("sbuf", [128, B], "bfloat16"),
    "wts": ("sbuf", [128, B], "bfloat16"),
    "dys": ("sbuf", [128, N * B], "bfloat16"),
    "dyts": ("sbuf", [128, N * B], "bfloat16"),
    "xg": ("sbuf", [128, N * B], "bfloat16"),
    "pbs": ("sbuf", [128, 9 * B], "bfloat16"),
    "pl": ("sbuf", [128, 4 * B], "bfloat16"),
    "ub": ("sbuf", [128, 3 * B], "bfloat16"),
    "upb": ("sbuf", [128, 9 * B], "bfloat16"),
    "dxo": ("sbuf", [128, B], "bfloat16"),
    "dwo": ("sbuf", [128, B], "bfloat16"),
    "pb0": ("psum", [128, 512], "float32"),
    "pb1": ("psum", [128, 512], "float32"),
    "pb2": ("psum", [128, 512], "float32"),
    "pacc": ("psum", [128, 512], "float32"),
    "pdw": ("psum", [128, 512], "float32"),
}
SEMAPHORES = ["lx", "lw", "ld0", "ld1", "lt0", "lt1", "mb0", "mb1", "mb2", "mo", "md", "vc", "vc2", "vd", "va",
              "xr0", "xr1", "xr2", "xr3", "xf0", "xf1", "xf2", "xf3", "pr0", "pr1", "pr2", "pr3",
              "ux", "uy", "up", "sent", "sdw", "sdx"]

_CACHE = {}


def _bits(mask):
    return [b for b in range(32) if (mask >> b) & 1]


def _mk(bits):
    m = 0
    for b in bits:
        m |= 1 << b
    return m


def _plan(cores, topo):
    key = tuple(cores)
    if key in _CACHE:
        return _CACHE[key]
    ranks = list(cores)
    hosts = sorted(set(topo.host(c) for c in ranks))
    world = range((max(hosts) + 1) * topo.CORES_PER_HOST)
    chips = sorted(set(topo.chip(c) for c in ranks))

    def on(h, q):
        return [c for c in ranks if topo.host(c) == h and topo.chip(c) == chips[q]]

    def inhost(h):
        return [c for c in ranks if topo.host(c) == h]

    def rackmate(h):
        return [k for k in hosts if k != h and topo.rack(k) == topo.rack(h)][0]

    def cabled(h):
        return [k for k in hosts if topo.rack(k) != topo.rack(h) and topo.may_write(inhost(h)[0], inhost(k)[0])][0]

    def pos(h):
        return 0 if len(inhost(h)) < len(inhost(rackmate(h))) else 1

    relay = {}
    for h in hosts:
        for q in (0, 1):
            other = on(h, 1 - q)[0]
            mine = on(h, q)[0]
            cand = [c for c in world if topo.host(c) == h and topo.chip(c) == chips[q] and c not in ranks
                    and topo.may_write(c, other)]
            relay[(h, q, "A")] = [c for c in cand if topo.die(c) == topo.die(mine)][0]
            relay[(h, q, "B")] = [c for c in cand if topo.die(c) != topo.die(mine)][0]

    arr = {}
    calls = {}

    def add(core, wait, transfers):
        calls.setdefault(core, []).append((wait, transfers))
        for t in transfers:
            n = len(_bits(t["mask"]))
            for d in t["to"]:
                arr[(d, t["sem"])] = arr.get((d, t["sem"]), 0) + n
            arr[(core, "sent")] = arr.get((core, "sent"), 0) + n

    def lanes(core, dests):
        m = ~0
        for d in dests:
            m &= topo.mask(core, d)
        return m

    def split(core, dests):
        onc = [d for d in dests if topo.host(d) == topo.host(core) and topo.chip(d) == topo.chip(core)]
        off = [d for d in dests if d not in onc]
        lo = lanes(core, off)
        hi = (lanes(core, onc) & ~lo) if onc else 0
        return off, onc, _bits(lo), _bits(hi)

    xsrc = {}
    for h in hosts:
        for q in (0, 1):
            xsrc[(h, q)] = on(h, q) + on(cabled(h), q)
    width = [len(xsrc[(hosts[0], q)]) for q in (0, 1)]
    xoff = [0, width[0] * B, 2 * width[0] * B, (2 * width[0] + width[1]) * B]
    xunits = []
    for h in hosts:
        for q in (0, 1):
            oth = on(rackmate(h), 1 - q) + on(h, 1 - q)
            moved = [c for c in oth if pos(topo.host(c)) == 0] if len(oth) > 2 else []
            for ab, to in (("A", on(rackmate(h), q) + moved + on(h, q)), ("B", [c for c in oth if c not in moved])):
                xunits.append({"core": relay[(h, q, ab)], "srcs": xsrc[(h, q)], "dests": to, "k": 2 * q + pos(h)})

    units = []
    for e in hosts:
        if pos(e) != 0:
            continue
        o = rackmate(e)
        for q in (0, 1):
            srcs = on(e, q) + on(o, q)
            fe, fo = inhost(cabled(e)), inhost(cabled(o))
            ne = [c for c in inhost(e) if c not in srcs]
            no = [c for c in inhost(o) if c not in srcs]
            two = len(on(o, q)) > 1
            for hh, ab, to in ((e, "B", fe[0:2]), (e, "A", fe[2:] + ne + ([] if two else on(e, q))),
                               (o, "B", fo[0:1] + no[0:1]), (o, "A", fo[1:] + no[1:] + (on(e, q) if two else []) + on(o, q))):
                units.append({"core": relay[(hh, q, ab)], "srcs": srcs, "dests": to, "q": q})

    info = {}
    for c in ranks:
        h, q = topo.host(c), chips.index(topo.chip(c))
        far = cabled(h)
        xto = [relay[(far, q, "A")], relay[(far, q, "B")], relay[(h, q, "A")], relay[(h, q, "B")]]
        off, onc, lo, hi = split(c, xto)
        add(c, None, [
            {"srcs": [("xs", 0, B)], "to": off, "dst": ("ub", xsrc[(far, q)].index(c) * B, B), "mask": _mk(lo), "sem": "uy"},
            {"srcs": [("xs", 0, B)], "to": onc, "dst": ("ub", xsrc[(h, q)].index(c) * B, B), "mask": _mk(hi), "sem": "ux"},
        ])
        mine = [u for u in units if c in u["srcs"]]
        mine.sort(key=lambda u: len([d for d in u["dests"] if d != c]))
        bundles = [[d for d in u["dests"] if d != c] for u in mine]
        start = [sum(len(b) for b in bundles[:k]) * B for k in range(len(mine))]
        for wd in sorted(set(len(b) for b in bundles)):
            trs = []
            for grp, bl in ((False, lo), (True, hi)):
                ks = [k for k in range(len(mine)) if (mine[k]["core"] in onc) == grp and len(bundles[k]) == wd]
                for i, k in enumerate(ks):
                    per = len(bl) // len(ks)
                    trs.append({"srcs": [("pbs", start[k], wd * B)], "to": [mine[k]["core"]],
                                "dst": ("upb", mine[k]["srcs"].index(c) * W3, wd * B),
                                "mask": _mk(bl[i * per:(i + 1) * per]), "sem": "up"})
            add(c, None, trs)
        info[c] = {"order": [d for b in bundles for d in b]}

    for u in xunits:
        rc, k = u["core"], u["k"]
        n = len(u["srcs"])
        own = len([s for s in u["srcs"] if topo.host(s) == topo.host(rc)])
        off, onc, lo, hi = split(rc, u["dests"])
        for wait, sem, c0, m in (("ux", "xr%d" % k, 0, own), ("uy", "xf%d" % k, own, n - own)):
            src, dst = ("ub", c0 * B, m * B), ("xg", xoff[k] + c0 * B, m * B)
            trs = [{"srcs": [src], "to": off, "dst": dst, "mask": _mk(lo), "sem": sem}]
            if onc and (wait == "uy" or own > 1):
                trs.append({"srcs": [src], "to": onc, "dst": dst, "mask": _mk(hi[0:4 * len(onc)]), "sem": sem})
            add(rc, wait, trs)
    for u in units:
        rc = u["core"]
        off, onc, lo, hi = split(rc, u["dests"])
        per = len(lo) // len(off)
        trs = []
        for d in u["dests"]:
            srcs = []
            for si, s in enumerate(u["srcs"]):
                if s != d:
                    srcs.append(("upb", si * W3 + [x for x in u["dests"] if x != s].index(d) * B, B))
            slot = 2 * (1 if topo.rack(topo.host(d)) == topo.rack(topo.host(rc)) else 0) + u["q"]
            if d in off:
                i = off.index(d)
                m = _mk(lo[i * per:(i + 1) * per])
            else:
                i = onc.index(d)
                m = _mk(hi[4 * i:4 * i + 4])
            trs.append({"srcs": srcs, "to": [d], "dst": ("pl", slot * B, B), "mask": m, "sem": "pr%d" % slot})
        add(rc, "up", trs)

    for c in ranks:
        h, q = topo.host(c), chips.index(topo.chip(c))
        groups = []
        for early in (True, False):
            for (hh, qq) in ((h, q), (rackmate(h), q), (h, 1 - q), (rackmate(h), 1 - q)):
                k = 2 * qq + pos(hh)
                parts = [(ranks.index(s), xoff[k] + i * B) for i, s in enumerate(xsrc[(hh, qq)])
                         if s != c and (topo.host(s) == hh) == early]
                if parts:
                    groups.append((("xr%d" if early else "xf%d") % k, parts))
        info[c]["xgroups"] = groups
    out = {"calls": calls, "arr": arr, "info": info}
    _CACHE[key] = out
    return out


def _ap(T, spec):
    buf, c0, n = spec
    return T[buf][:, c0:c0 + n]


def _issue(g, core, T, topo, transfers):
    out = []
    for t in transfers:
        ids = []
        for d in t["to"]:
            rid, pid = topo.addr(d, core)
            ids.append(DstId(rid=rid, pnc=pid))
        out.append(RemoteDMATransfer(dst_ids=ids, dma_engine_mask=t["mask"], remote_sem=T.sem[t["sem"]],
                                     srcs=[_ap(T, s) for s in t["srcs"]], dsts=[_ap(T, t["dst"]) for _ in t["to"]],
                                     alu_op=1 if len(t["srcs"]) > 1 else 0))
    g.remote_dma_fused(out, local_sem=T.sem.sent)


def rank_program(g, core, T, topo):
    plan = _plan(T.cores, topo)
    calls = plan["calls"].get(core)
    if calls is None:
        return
    arr, S = plan["arr"], T.sem
    r = T.rank_of(core)

    if r is None:
        for sem, trs in calls:
            g.wait_ge(S[sem], arr[(core, sem)])
            _issue(g, core, T, topo, trs)
        g.wait_ge(S.sent, arr[(core, "sent")])
        return

    info = plan["info"][core]
    sy, sc, te, ve = g.sync, g.scalar, g.tensor, g.vector
    H = (N // 2) * B

    sy.dma_start(T.xs[:], T.x[:]).then_inc(S.lx, 16)
    sc.dma_start(T.wts[:], T.wt[:]).then_inc(S.lw, 16)
    sy.dma_start(T.dys[:, 0:H], T.dy[:, 0:H]).then_inc(S.ld0, 16)
    sc.dma_start(T.dys[:, H:N * B], T.dy[:, H:N * B]).then_inc(S.ld1, 16)
    sy.dma_start(T.dyts[:, 0:H], T.dyt[:, 0:H]).then_inc(S.lt0, 16)
    sc.dma_start(T.dyts[:, H:N * B], T.dyt[:, H:N * B]).then_inc(S.lt1, 16)

    g.wait_ge(S.lx, 16)
    _issue(g, core, T, topo, calls[0][1])
    g.wait_ge(S.vc, 2)
    _issue(g, core, T, topo, calls[1][1])
    g.wait_ge(S.vc2, 1)
    _issue(g, core, T, topo, calls[2][1])

    te.wait_ge(S.lw, 16)
    te.wait_ge(S.ld0, 16)
    te.wait_ge(S.ld1, 16)
    for n, d in enumerate(info["order"]):
        k, i, j = n // 3, n % 3, T.rank_of(d)
        te.matmul(T["pb%d" % k][:, i * B:(i + 1) * B], T.wts[:], T.dys[:, j * B:(j + 1) * B], True, True).then_inc(S["mb%d" % k], 1)
    te.matmul(T.pacc[:, 0:B], T.wts[:], T.dys[:, r * B:(r + 1) * B], True, True).then_inc(S.mo, 1)
    te.wait_ge(S.lx, 16)
    te.wait_ge(S.lt0, 16)
    te.wait_ge(S.lt1, 16)
    te.matmul(T.pdw[:, 0:B], T.xs[:], T.dyts[:, r * B:(r + 1) * B], True, False).then_inc(S.md, 1)
    left = N - 1
    for sem, parts in info["xgroups"]:
        te.wait_ge(S[sem], arr[(core, sem)])
        for j, col in parts:
            left -= 1
            te.matmul(T.pdw[:, 0:B], T.xg[:, col:col + B], T.dyts[:, j * B:(j + 1) * B], False, left == 0).then_inc(S.md, 1)

    for k in range(3):
        ve.wait_ge(S["mb%d" % k], 3)
        ve.tensor_copy(T.pbs[:, k * W3:(k + 1) * W3], T["pb%d" % k][:, 0:W3]).then_inc(S.vc if k < 2 else S.vc2, 1)
    ve.wait_ge(S.md, N)
    ve.tensor_copy(T.dwo[:], T.pdw[:, 0:B]).then_inc(S.vd, 1)
    ve.wait_ge(S.mo, 1)
    for i, slot in enumerate((2, 3, 0, 1)):
        sem = "pr%d" % slot
        ve.wait_ge(S[sem], arr[(core, sem)])
        if i:
            ve.wait_ge(S.va, i)
        dst = T.dxo[:] if i == 3 else T.pacc[:, (i + 1) * B:(i + 2) * B]
        ve.tensor_tensor(dst, T.pacc[:, i * B:(i + 1) * B], T.pl[:, slot * B:(slot + 1) * B], AluOpType.add).then_inc(S.va, 1)

    sy.wait_ge(S.vd, 1)
    sy.dma_start(T.dw[:], T.dwo[:]).then_inc(S.sdw, 16)
    sy.wait_ge(S.sdw, 16)
    sc.wait_ge(S.va, 4)
    sc.dma_start(T.dx[:], T.dxo[:]).then_inc(S.sdx, 16)
    sc.wait_ge(S.sdx, 16)
    g.wait_ge(S.sent, arr[(core, "sent")])
